import numpy as np
import ml_dtypes


def mxq(x, axis, fmt="e4m3"):
    dtype, down = {"e4m3": (ml_dtypes.float8_e4m3fn, 7), "e5m2": (ml_dtypes.float8_e5m2, 14)}[fmt]
    v = np.moveaxis(np.asarray(x, np.float32).astype(ml_dtypes.bfloat16).astype(np.float64), axis, -1)
    blocks = v.reshape(v.shape[:-1] + (-1, 32))
    amax = np.abs(blocks).max(-1, keepdims=True)
    byte = np.maximum(np.where(amax > 0, np.frexp(amax)[1] - 1 + 127, 0) - down, 1)
    scale = np.exp2(byte - 127.0)
    codes = (blocks / scale).astype(np.float32).astype(dtype).astype(np.float64)
    return np.moveaxis((codes * scale).reshape(v.shape), -1, axis)


WIDE = False


def mx_kscale(k):
    if not WIDE:
        return np.ones(k)
    levels = np.array([10, -10, 5, -5, 0])
    if k % 512:
        return np.exp2(np.random.permutation(np.resize(levels, k // 32))).repeat(32)
    a = np.empty((k // 512, 16))
    for p in range(k // 512):
        a[p, :8] = np.random.permutation(np.resize(levels, 8))
        for g in range(8):
            far = levels[np.abs(levels - a[p, g]) >= 10]
            a[p, g + 8] = far[np.random.randint(len(far))]
    return np.exp2(a.ravel()).repeat(32)


BF16 = ml_dtypes.bfloat16


def bf(x):
    return np.asarray(x, np.float32).astype(BF16)


def f64(x):
    return np.asarray(x).astype(np.float64)

def planes(Y):
    n, m = Y.shape
    b = f64(bf(Y)).reshape(n // 32, 32, m)
    amax = np.abs(b).max(1)
    byte = np.clip(np.where(amax > 0, np.frexp(amax)[1] - 1 + 127 - 7, 1), 1, 254)
    codes = (b * np.exp2(127.0 - byte)[:, None, :]).reshape(n, m).astype(np.float32).astype(ml_dtypes.float8_e4m3fn).view(np.uint8)
    words = codes.reshape(n // 512, 128, 4, m).transpose(0, 1, 3, 2)
    return np.ascontiguousarray(words), np.ascontiguousarray(byte.astype(np.uint8).reshape(n // 512, 16, m))


N, P, D, R, F = 4, 512, 1024, 512, 1024


def sigmoid(v):
    return 1.0 / (1.0 + np.exp(-v))


def setup_inputs():
    s, c = mx_kscale(R), mx_kscale(D)
    return {
        "x": bf(np.random.standard_normal((N, P, D)) * c),
        "a": bf(np.random.standard_normal((N, D, R)) * s),
        "u": bf(np.random.standard_normal((N, R, F)) * (1.5 / np.sqrt(R)) / s[:, None]),
        "w": bf(np.random.standard_normal((D, F)) * (2.0 / np.sqrt(D)) / c[:, None]),
        "bias": bf(np.random.standard_normal(F) * 0.3),
    }


def modulated_weight(a, u, w):
    t = mxq(a, 2, "e4m3") @ mxq(u, 1, "e4m3")
    return w[None, :, :] * sigmoid(t)


def core(x, a, u, w, bias):
    wm = modulated_weight(f64(a), f64(u), f64(w))
    h = mxq(f64(x), 2, "e4m3") @ mxq(wm, 1, "e4m3")
    h = h + f64(bias)[None, None, :]
    return np.maximum(h, 0.2 * h)


def reference(x, a, u, w, bias):
    R_out = core(x, a, u, w, bias)
    words, scales = planes(np.moveaxis(R_out, 1, 0).reshape(512, -1))
    return R_out, words, scales

@@ -1,0 +1,340 @@
+from contextlib import ExitStack
+
+import concourse.mybir as mybir
+from concourse.masks import make_identity
+
+N, TOK, D, R, F = 4, 512, 1024, 512, 1024
+FLOPS = N * (2 * D * R * F + 2 * TOK * D * F)
+
+F32 = mybir.dt.float32
+BF16 = mybir.dt.bfloat16
+I32 = mybir.dt.int32
+U32 = mybir.dt.uint32
+U8 = mybir.dt.uint8
+FP8X4 = mybir.dt.float8_e4m3fn_x4
+ACT = mybir.ActivationFunctionType
+ALU = mybir.AluOpType
+
+P = 128
+PACK = 4
+GROUPS = D // (P * PACK)
+CH = 128
+STEPS_PER_SAMPLE = F // CH
+STEPS = N * STEPS_PER_SAMPLE
+FV = 96
+SLOPE = 0.2
+FIRST_RANGES = [(0, 256), (256, 512), (512, 1024)]
+
+
+def tile_factorizedmultiplicativemodulationinr_x1_kernel(tc, x, a, u, w, bias, out_0, out_1, out_2):
+    nc = tc.nc
+    with ExitStack() as ctx:
+        keep = ctx.enter_context(tc.tile_pool(name="keep", bufs=1))
+        ring = ctx.enter_context(tc.tile_pool(name="ring", bufs=2))
+        psum = ctx.enter_context(tc.psum_pool(name="psum", bufs=1))
+        ctx.enter_context(tc.manual_schedule())
+
+        def bank(tag, shape, dtype):
+            return psum.tile(shape, dtype, name=tag, tag=tag)
+
+        ident32 = keep.tile([P, P], F32, name="ident32")
+        ident16 = keep.tile([P, P], BF16, name="ident16")
+        ones16 = keep.tile([P, P], BF16, name="ones16")
+        bias_row = keep.tile([P, F], BF16, name="bias_row")
+        bias_all = keep.tile([P, F], BF16, name="bias_all")
+        warm = keep.tile([P, 1], F32, name="warm")
+        wm_bf = keep.tile([P, GROUPS, CH, PACK], BF16, name="wm_bf", align_bytes=64)
+        out_words = keep.tile([P, N * F], U32, name="out_words", align_bytes=64)
+        out_scales = keep.tile([P, N * F], U8, name="out_scales", align_bytes=64)
+        a_raw = [keep.tile([P, GROUPS, PACK * R], BF16, name="a_raw%d" % n) for n in range(N)]
+        x_raw = [keep.tile([P, PACK, D], BF16, name="x_raw%d" % n) for n in range(N)]
+        u_ranges = [FIRST_RANGES] + [[(0, F)]] * (N - 1)
+        u_raw = {}
+        for n in range(N):
+            for lo, hi in u_ranges[n]:
+                u_raw[n, lo] = keep.tile([P, PACK, hi - lo], BF16, name="u_raw%d_%d" % (n, lo))
+        w_raw = {}
+        for lo, hi in FIRST_RANGES:
+            w_raw[lo] = keep.tile([P, GROUPS, PACK, hi - lo], BF16, name="w_raw%d" % lo)
+
+        def find(ranges, col):
+            return [lo for lo, hi in ranges if lo <= col < hi][0]
+
+        def load_a(n, g):
+            rows = a[n, g * P * PACK:(g + 1) * P * PACK, :]
+            nc.sync.dma_start(out=a_raw[n][:, g, :], in_=rows.rearrange("(m t) r -> m (t r)", t=PACK))
+
+        def load_x(n, t0, t1):
+            view = x[n].rearrange("(m t) d -> m t d", t=PACK)
+            nc.sync.dma_start(out=x_raw[n][:, t0:t1, :], in_=view[:, t0:t1, :])
+
+        def load_u(n, i):
+            lo, hi = u_ranges[n][i]
+            view = u[n].rearrange("(p j) f -> p j f", j=PACK)
+            nc.sync.dma_start(out=u_raw[n, lo][:], in_=view[:, :, lo:hi])
+
+        def load_w(i):
+            lo, hi = FIRST_RANGES[i]
+            for g in range(GROUPS):
+                view = w[g * P * PACK:(g + 1) * P * PACK, :].rearrange("(p t) f -> p t f", t=PACK)
+                nc.sync.dma_start(out=w_raw[lo][:, g, :, :], in_=view[:, :, lo:hi])
+
+        turned, grouped, codes, scales = {}, {}, {}, {}
+
+        def turn(kind, n, j, tag):
+            tile = bank(tag, [P, 2, 2, P], F32)
+            for i in range(2):
+                if kind == "a":
+                    t = 2 * (j % 2) + i
+                    words = a_raw[n][:, j // 2, t * R:(t + 1) * R].bitcast(F32)
+                else:
+                    words = x_raw[n][:, j, i * P * PACK:(i + 1) * P * PACK].bitcast(F32)
+                for half in range(2):
+                    nc.tensor.transpose(tile[:, i, half, :], words[:, half:2 * P:2], ident32[:])
+            turned[kind, n, j] = tile
+
+        def turn_out(kind, n, j, on_vector):
+            tile = ring.tile([P, 2 * P * PACK], BF16, name="grouped", tag="grouped", bufs=4, align_bytes=64)
+            dst = tile[:].bitcast(F32).rearrange("p (i m h) -> p i m h", i=2, h=2)
+            src = turned[kind, n, j][:].rearrange("p i h m -> p i m h")
+            if on_vector:
+                nc.vector.tensor_copy(out=dst, in_=src)
+            else:
+                nc.scalar.copy(out=dst, in_=src)
+            grouped[kind, n, j] = tile
+
+        def turn_quant(kind, n, j):
+            if j == 0:
+                codes[kind, n] = ring.tile([P, 8 * P], U32, name=kind + "_codes", tag=kind + "_codes", align_bytes=64)
+                scales[kind, n] = ring.tile([P, 8 * P], U8, name=kind + "_scales", tag=kind + "_scales", align_bytes=64)
+            cols = slice(2 * P * j, 2 * P * (j + 1))
+            nc.vector.quantize_mx(out=codes[kind, n][:, cols].bitcast(FP8X4), scales=scales[kind, n][:, cols],
+                                  in_=grouped[kind, n, j][:])
+
+        u_bf, t_bank, sig, w_bank, h_bank, z_sb, y_sb, y_bf = {}, {}, {}, {}, {}, {}, {}, {}
+
+        def interleave_views(dst, src):
+            return (dst.rearrange("p (c i t) -> p c t i", i=4, t=PACK), src.rearrange("p t (c i) -> p c t i", i=4))
+
+        def u_interleave(s, on_vector):
+            n, col = s // STEPS_PER_SAMPLE, (s % STEPS_PER_SAMPLE) * CH
+            lo = find(u_ranges[n], col)
+            tile = ring.tile([P, CH * PACK], BF16, name="u_bf", tag="u_bf", bufs=3, align_bytes=64)
+            dst, src = interleave_views(tile[:], u_raw[n, lo][:, :, col - lo:col - lo + CH])
+            if on_vector:
+                nc.vector.tensor_copy(out=dst, in_=src)
+            else:
+                nc.scalar.copy(out=dst, in_=src)
+            u_bf[s] = tile
+
+        def u_quant(s):
+            codes["u", s] = ring.tile([P, CH], U32, name="u_codes", tag="u_codes", bufs=3, align_bytes=64)
+            scales["u", s] = ring.tile([P, CH], U8, name="u_scales", tag="u_scales", bufs=3, align_bytes=64)
+            nc.vector.quantize_mx(out=codes["u", s][:].bitcast(FP8X4), scales=scales["u", s][:], in_=u_bf[s][:])
+
+        def stage1(s):
+            n = s // STEPS_PER_SAMPLE
+            for g in range(GROUPS):
+                tile = bank("t%d" % ((GROUPS * s + g) % 3), [P, PACK, CH], F32)
+                for t in range(PACK):
+                    cols = slice((g * PACK + t) * P, (g * PACK + t + 1) * P)
+                    nc.tensor.matmul_mx(out=tile[:, t, :], lhsT=codes["a", n][:, cols].bitcast(FP8X4),
+                                        lhsT_scale=scales["a", n][:, cols], rhs=codes["u", s][:].bitcast(FP8X4),
+                                        rhs_scale=scales["u", s][:], start=True, stop=True)
+                t_bank[s, g] = tile
+
+        def sigmoid(s):
+            sig[s] = ring.tile([P, GROUPS, CH, PACK], F32, name="sig", tag="sig", bufs=3)
+            for g in range(GROUPS):
+                nc.scalar.activation(out=sig[s][:, g, :, :], in_=t_bank[s, g][:].rearrange("p t f -> p f t"),
+                                     func=ACT.Sigmoid)
+
+        def w_chunk(s):
+            col = (s % STEPS_PER_SAMPLE) * CH
+            lo = find(FIRST_RANGES, col)
+            return w_raw[lo][:, :, :, col - lo:col - lo + CH]
+
+        def w_to_psum(s):
+            tile = bank("w%d" % (s % 2), [P, GROUPS, PACK, FV], BF16)
+            for g in range(GROUPS):
+                nc.tensor.matmul(out=tile[:, g, :, :], lhsT=ident16[:], rhs=w_chunk(s)[:, g, :, :FV], start=True, stop=True)
+            w_bank[s] = tile
+
+        def gate_vector(s):
+            nc.vector.tensor_tensor(out=wm_bf[:, :, :FV, :], in0=sig[s][:, :, :FV, :],
+                                    in1=w_bank[s][:].rearrange("p g t f -> p g f t"), op=ALU.mult)
+
+        def gate_gpsimd(s):
+            nc.gpsimd.tensor_tensor(out=wm_bf[:, :, FV:, :], in0=sig[s][:, :, FV:, :],
+                                    in1=w_chunk(s)[:, :, :, FV:].rearrange("p g t f -> p g f t"), op=ALU.mult)
+
+        def wm_quant(s):
+            codes["wm", s] = ring.tile([P, GROUPS * CH], U32, name="wm_codes", tag="wm_codes", bufs=3, align_bytes=64)
+            scales["wm", s] = ring.tile([P, GROUPS * CH], U8, name="wm_scales", tag="wm_scales", bufs=3, align_bytes=64)
+            nc.vector.quantize_mx(out=codes["wm", s][:].bitcast(FP8X4), scales=scales["wm", s][:],
+                                  in_=wm_bf[:].rearrange("p g f t -> p (g f t)"))
+
+        def stage2(s):
+            n = s // STEPS_PER_SAMPLE
+            tile = bank("h%d" % (s % 2), [P, PACK, CH], F32)
+            for t in range(PACK):
+                for g in range(GROUPS):
+                    cols = slice((t * GROUPS + g) * P, (t * GROUPS + g + 1) * P)
+                    wm_cols = slice(g * CH, (g + 1) * CH)
+                    nc.tensor.matmul_mx(out=tile[:, t, :], lhsT=codes["x", n][:, cols].bitcast(FP8X4),
+                                        lhsT_scale=scales["x", n][:, cols],
+                                        rhs=codes["wm", s][:, wm_cols].bitcast(FP8X4),
+                                        rhs_scale=scales["wm", s][:, wm_cols], start=(g == 0), stop=(g == GROUPS - 1))
+            h_bank[s] = tile
+
+        def add_bias(s):
+            col = (s % STEPS_PER_SAMPLE) * CH
+            z_sb[s] = ring.tile([P, PACK, CH], F32, name="z_sb", tag="z_sb")
+            nc.vector.tensor_tensor(out=z_sb[s][:], in0=h_bank[s][:],
+                                    in1=bias_all[:, col:col + CH].unsqueeze(1).to_broadcast([P, PACK, CH]), op=ALU.add)
+
+        def y_view(s):
+            return y_sb[s // 2][:, :, (s % 2) * CH:(s % 2 + 1) * CH]
+
+        def leaky(s):
+            if s % 2 == 0:
+                y_sb[s // 2] = ring.tile([P, PACK, 2 * CH], F32, name="y_sb", tag="y_sb", bufs=4)
+            nc.vector.scalar_tensor_tensor(out=y_view(s), in0=z_sb[s][:], scalar=SLOPE, in1=z_sb[s][:],
+                                           op0=ALU.mult, op1=ALU.max)
+
+        def y_interleave(s):
+            y_bf[s] = ring.tile([P, CH * PACK], BF16, name="y_bf", tag="y_bf", bufs=3, align_bytes=64)
+            dst, src = interleave_views(y_bf[s][:], y_view(s))
+            nc.scalar.copy(out=dst, in_=src)
+
+        def y_quant(s):
+            cols = slice(s * CH, (s + 1) * CH)
+            nc.vector.quantize_mx(out=out_words[:, cols].bitcast(FP8X4), scales=out_scales[:, cols], in_=y_bf[s][:])
+
+        def store_y(s0, s1):
+            n, col = s0 // STEPS_PER_SAMPLE, (s0 % STEPS_PER_SAMPLE) * CH
+            view = out_0[n].rearrange("(p t) f -> p t f", t=PACK)
+            off = (s0 % 2) * CH
+            width = (s1 - s0) * CH
+            nc.sync.dma_start(out=view[:, :, col:col + width], in_=y_sb[s0 // 2][:, :, off:off + width])
+
+        def store_words(s0, s1):
+            view = out_1[0].rearrange("p m t -> p (m t)").bitcast(I32)
+            cols = slice(s0 * CH, s1 * CH)
+            nc.sync.dma_start(out=view[:, cols], in_=out_words[:, cols].bitcast(I32))
+
+        def store_scales(s0, s1, queues):
+            cols = slice(s0 * CH, s1 * CH)
+            for q in range(4):
+                queues[q].dma_start(out=out_2[0, 4 * q:4 * q + 4, cols].bitcast(I32),
+                                    in_=out_scales[32 * q:32 * q + 4, cols].bitcast(I32))
+
+        load_a(0, 0)
+        load_u(0, 0)
+        load_a(0, 1)
+        load_w(0)
+        load_u(0, 1)
+        load_x(0, 0, 2)
+        load_x(0, 2, 4)
+        make_identity(nc, ident32[:])
+        make_identity(nc, ident16[:])
+        nc.gpsimd.memset(ones16[:], 1.0)
+        nc.gpsimd.memset(bias_row[:], 0.0)
+        nc.vector.memset(warm[:], 0.0)
+        nc.scalar.activation(out=warm[:], in_=warm[:], func=ACT.Sigmoid)
+        nc.sync.dma_start(out=bias_row[0:1, :], in_=bias.unsqueeze(0))
+        load_a(1, 0)
+        load_w(1)
+        load_u(0, 2)
+        load_a(1, 1)
+        load_w(2)
+
+        turn("a", 0, 0, "turn")
+        turn("a", 0, 1, "h0")
+        turn("a", 0, 2, "h1")
+        turn("a", 0, 3, "w1")
+        u_interleave(0, True)
+        turn_out("a", 0, 0, False)
+        turn_out("a", 0, 1, True)
+        u_quant(0)
+        turn_quant("a", 0, 0)
+        turn_out("a", 0, 2, False)
+        turn_quant("a", 0, 1)
+        turn_out("a", 0, 3, True)
+        u_interleave(1, False)
+        turn_quant("a", 0, 2)
+        u_quant(1)
+        turn_quant("a", 0, 3)
+
+        turns = {-1: [("x", 0, 0, "turn"), ("x", 0, 1, "h0")], 0: [("x", 0, 2, "h1"), ("x", 0, 3, "turn")]}
+        for n in range(1, N):
+            for j in range(4):
+                turns[STEPS_PER_SAMPLE * (n - 1) + 1 + j] = [("a", n, j, "turn")]
+                turns[STEPS_PER_SAMPLE * (n - 1) + 5 + j] = [("x", n, j, "turn")]
+
+        def live(s):
+            return 0 <= s < STEPS
+
+        for s in range(-2, STEPS + 5):
+            early = s < 3
+            if live(s - 2):
+                stage2(s - 2)
+            if live(s + 1):
+                w_to_psum(s + 1)
+                sigmoid(s + 1)
+            if live(s):
+                gate_gpsimd(s)
+            if live(s - 3):
+                add_bias(s - 3)
+            if live(s):
+                gate_vector(s)
+            if s == 1:
+                spread = bank("h1", [P, F], BF16)
+                for half in range(2):
+                    cols = slice(half * 512, (half + 1) * 512)
+                    nc.tensor.matmul(out=spread[:, cols], lhsT=ones16[:], rhs=bias_row[:, cols], start=True, stop=True)
+            for kind, n, j, tag in turns.get(s, []):
+                turn(kind, n, j, tag)
+            if live(s + 2):
+                stage1(s + 2)
+            if live(s + 4):
+                u_interleave(s + 4, False)
+            for kind, n, j, tag in turns.get(s, []):
+                turn_out(kind, n, j, early)
+            if s == 1:
+                nc.scalar.copy(out=bias_all[:], in_=spread[:])
+            if live(s - 3):
+                leaky(s - 3)
+            for kind, n, j, tag in turns.get(s - 1, []):
+                turn_quant(kind, n, j)
+            if live(s + 3) and s + 3 >= 2:
+                u_quant(s + 3)
+            if live(s - 4):
+                y_quant(s - 4)
+            if live(s):
+                wm_quant(s)
+            if live(s - 3):
+                y_interleave(s - 3)
+
+            done = s - 3
+            if live(done) and done >= STEPS - 2:
+                store_y(done, done + 1)
+            elif live(done) and done % 2 == 1:
+                store_y(done - 1, done + 1)
+            packed = s - 4
+            if packed == STEPS - 2:
+                store_words(STEPS - 4, STEPS - 1)
+                store_scales(0, STEPS - 1, [nc.sync] * 4)
+            elif packed == STEPS - 1:
+                store_words(STEPS - 1, STEPS)
+                store_scales(STEPS - 1, STEPS, [nc.sync, nc.scalar, nc.sync, nc.scalar])
+            elif live(packed) and packed % 4 == 3:
+                store_words(packed - 3, packed + 1)
+
+            ahead, phase = s // STEPS_PER_SAMPLE + 1, s % STEPS_PER_SAMPLE
+            if 1 <= ahead < N and phase == 0:
+                load_u(ahead, 0)
+                load_x(ahead, 0, PACK)
+            if 1 <= ahead < N - 1 and phase == 4:
+                load_a(ahead + 1, 0)
+                load_a(ahead + 1, 1)

@@ -21,9 +21,11 @@ GROUPS = D // (P * PACK)
 CH = 128
 STEPS_PER_SAMPLE = F // CH
 STEPS = N * STEPS_PER_SAMPLE
-FV = 96
+GW = 320
+VW = GROUPS * CH * PACK - GW
+TW = 2 * P * PACK
 SLOPE = 0.2
-FIRST_RANGES = [(0, 256), (256, 512), (512, 1024)]
+FIRST_RANGES = [(0, 256), (256, 512), (512, 768), (768, 1024)]
 
 
 def tile_factorizedmultiplicativemodulationinr_x1_kernel(tc, x, a, u, w, bias, out_0, out_1, out_2):
@@ -43,16 +45,13 @@ def tile_factorizedmultiplicativemodulationinr_x1_kernel(tc, x, a, u, w, bias, o
         bias_row = keep.tile([P, F], BF16, name="bias_row")
         bias_all = keep.tile([P, F], BF16, name="bias_all")
         warm = keep.tile([P, 1], F32, name="warm")
-        wm_bf = keep.tile([P, GROUPS, CH, PACK], BF16, name="wm_bf", align_bytes=64)
+        stage = keep.tile([P, 2 * TW + 2 * VW + GW], BF16, name="stage", align_bytes=64)
         out_words = keep.tile([P, N * F], U32, name="out_words", align_bytes=64)
         out_scales = keep.tile([P, N * F], U8, name="out_scales", align_bytes=64)
-        a_raw = [keep.tile([P, GROUPS, PACK * R], BF16, name="a_raw%d" % n) for n in range(N)]
-        x_raw = [keep.tile([P, PACK, D], BF16, name="x_raw%d" % n) for n in range(N)]
-        u_ranges = [FIRST_RANGES] + [[(0, F)]] * (N - 1)
-        u_raw = {}
-        for n in range(N):
-            for lo, hi in u_ranges[n]:
-                u_raw[n, lo] = keep.tile([P, PACK, hi - lo], BF16, name="u_raw%d_%d" % (n, lo))
+        u_ranges = [FIRST_RANGES] + [[(0, F // 2), (F // 2, F)]] * (N - 1)
+        a_raw, x_raw, u_raw = {}, {}, {}
+        for lo, hi in FIRST_RANGES:
+            u_raw[0, lo] = keep.tile([P, PACK, hi - lo], BF16, name="u_first%d" % lo)
         w_raw = {}
         for lo, hi in FIRST_RANGES:
             w_raw[lo] = keep.tile([P, GROUPS, PACK, hi - lo], BF16, name="w_raw%d" % lo)
@@ -60,16 +59,23 @@ def tile_factorizedmultiplicativemodulationinr_x1_kernel(tc, x, a, u, w, bias, o
         def find(ranges, col):
             return [lo for lo, hi in ranges if lo <= col < hi][0]
 
-        def load_a(n, g):
-            rows = a[n, g * P * PACK:(g + 1) * P * PACK, :]
-            nc.sync.dma_start(out=a_raw[n][:, g, :], in_=rows.rearrange("(m t) r -> m (t r)", t=PACK))
+        def load_a(n, j0, j1):
+            if j0 == 0:
+                a_raw[n] = ring.tile([P, GROUPS * PACK * R], BF16, name="a_raw", tag="a_raw")
+            g, t0, t1 = j0 // 2, 2 * (j0 % 2), 2 * (j0 % 2) + 2 * (j1 - j0)
+            rows = a[n, g * P * PACK:(g + 1) * P * PACK, :].rearrange("(m t) r -> m (t r)", t=PACK)
+            nc.sync.dma_start(out=a_raw[n][:, 2 * j0 * R:2 * j1 * R], in_=rows[:, t0 * R:t1 * R])
 
         def load_x(n, t0, t1):
+            if t0 == 0:
+                x_raw[n] = ring.tile([P, PACK, D], BF16, name="x_raw", tag="x_raw")
             view = x[n].rearrange("(m t) d -> m t d", t=PACK)
             nc.sync.dma_start(out=x_raw[n][:, t0:t1, :], in_=view[:, t0:t1, :])
 
         def load_u(n, i):
             lo, hi = u_ranges[n][i]
+            if n > 0:
+                u_raw[n, lo] = ring.tile([P, PACK, hi - lo], BF16, name="u_raw", tag="u_raw", bufs=4)
             view = u[n].rearrange("(p j) f -> p j f", j=PACK)
             nc.sync.dma_start(out=u_raw[n, lo][:], in_=view[:, :, lo:hi])
 
@@ -79,112 +85,136 @@ def tile_factorizedmultiplicativemodulationinr_x1_kernel(tc, x, a, u, w, bias, o
                 view = w[g * P * PACK:(g + 1) * P * PACK, :].rearrange("(p t) f -> p t f", t=PACK)
                 nc.sync.dma_start(out=w_raw[lo][:, g, :, :], in_=view[:, :, lo:hi])
 
-        turned, grouped, codes, scales = {}, {}, {}, {}
+        turned, grouped, quantised = {}, {}, {}
+
+        def copy_on(on_vector, dst, src):
+            if on_vector:
+                nc.vector.tensor_copy(out=dst, in_=src)
+            else:
+                nc.scalar.copy(out=dst, in_=src)
+
+        def quantise(tag, bufs, src):
+            width = src.shape[1] // PACK
+            codes = ring.tile([P, width], U32, name=tag + "_codes", tag=tag + "_codes", bufs=bufs, align_bytes=64)
+            scales = ring.tile([P, width], U8, name=tag + "_scales", tag=tag + "_scales", bufs=bufs, align_bytes=64)
+            nc.vector.quantize_mx(out=codes[:].bitcast(FP8X4), scales=scales[:], in_=src)
+            return codes, scales
+
+        def window(pair, col, width):
+            return pair[0][:, col:col + width], pair[1][:, col:col + width]
+
+        def mx(out, lhs, rhs, start, stop):
+            nc.tensor.matmul_mx(out=out, lhsT=lhs[0].bitcast(FP8X4), lhsT_scale=lhs[1], rhs=rhs[0].bitcast(FP8X4),
+                                rhs_scale=rhs[1], start=start, stop=stop)
 
         def turn(kind, n, j, tag):
             tile = bank(tag, [P, 2, 2, P], F32)
             for i in range(2):
                 if kind == "a":
-                    t = 2 * (j % 2) + i
-                    words = a_raw[n][:, j // 2, t * R:(t + 1) * R].bitcast(F32)
+                    words = a_raw[n][:, (2 * j + i) * R:(2 * j + i + 1) * R].bitcast(F32)
                 else:
                     words = x_raw[n][:, j, i * P * PACK:(i + 1) * P * PACK].bitcast(F32)
                 for half in range(2):
                     nc.tensor.transpose(tile[:, i, half, :], words[:, half:2 * P:2], ident32[:])
             turned[kind, n, j] = tile
 
-        def turn_out(kind, n, j, on_vector):
-            tile = ring.tile([P, 2 * P * PACK], BF16, name="grouped", tag="grouped", bufs=4, align_bytes=64)
-            dst = tile[:].bitcast(F32).rearrange("p (i m h) -> p i m h", i=2, h=2)
-            src = turned[kind, n, j][:].rearrange("p i h m -> p i m h")
-            if on_vector:
-                nc.vector.tensor_copy(out=dst, in_=src)
-            else:
-                nc.scalar.copy(out=dst, in_=src)
-            grouped[kind, n, j] = tile
+        def turn_out(kind, n, j, on_vector, dst):
+            copy_on(on_vector, dst.bitcast(F32).rearrange("p (i m h) -> p i m h", i=2, h=2),
+                    turned[kind, n, j][:].rearrange("p i h m -> p i m h"))
 
-        def turn_quant(kind, n, j):
-            if j == 0:
-                codes[kind, n] = ring.tile([P, 8 * P], U32, name=kind + "_codes", tag=kind + "_codes", align_bytes=64)
-                scales[kind, n] = ring.tile([P, 8 * P], U8, name=kind + "_scales", tag=kind + "_scales", align_bytes=64)
-            cols = slice(2 * P * j, 2 * P * (j + 1))
-            nc.vector.quantize_mx(out=codes[kind, n][:, cols].bitcast(FP8X4), scales=scales[kind, n][:, cols],
-                                  in_=grouped[kind, n, j][:])
+        def first_out(kind, j, on_vector):
+            grouped[kind, j] = ring.tile([P, TW], BF16, name="grouped", tag="grouped", bufs=4, align_bytes=64)
+            turn_out(kind, 0, j, on_vector, grouped[kind, j][:])
+
+        def first_quant(kind, j):
+            quantised[kind, 0, j] = window(quantise("first", 8, grouped[kind, j][:]), 0, 2 * P)
 
         u_bf, t_bank, sig, w_bank, h_bank, z_sb, y_sb, y_bf = {}, {}, {}, {}, {}, {}, {}, {}
 
         def interleave_views(dst, src):
             return (dst.rearrange("p (c i t) -> p c t i", i=4, t=PACK), src.rearrange("p t (c i) -> p c t i", i=4))
 
-        def u_interleave(s, on_vector):
-            n, col = s // STEPS_PER_SAMPLE, (s % STEPS_PER_SAMPLE) * CH
+        def u_interleave(k, on_vector):
+            n, col = 2 * k // STEPS_PER_SAMPLE, (2 * k % STEPS_PER_SAMPLE) * CH
             lo = find(u_ranges[n], col)
-            tile = ring.tile([P, CH * PACK], BF16, name="u_bf", tag="u_bf", bufs=3, align_bytes=64)
-            dst, src = interleave_views(tile[:], u_raw[n, lo][:, :, col - lo:col - lo + CH])
-            if on_vector:
-                nc.vector.tensor_copy(out=dst, in_=src)
-            else:
-                nc.scalar.copy(out=dst, in_=src)
-            u_bf[s] = tile
+            u_bf[k] = ring.tile([P, 2 * CH * PACK], BF16, name="u_bf", tag="u_bf", align_bytes=64)
+            dst, src = interleave_views(u_bf[k][:], u_raw[n, lo][:, :, col - lo:col - lo + 2 * CH])
+            copy_on(on_vector, dst, src)
 
-        def u_quant(s):
-            codes["u", s] = ring.tile([P, CH], U32, name="u_codes", tag="u_codes", bufs=3, align_bytes=64)
-            scales["u", s] = ring.tile([P, CH], U8, name="u_scales", tag="u_scales", bufs=3, align_bytes=64)
-            nc.vector.quantize_mx(out=codes["u", s][:].bitcast(FP8X4), scales=scales["u", s][:], in_=u_bf[s][:])
+        def u_quant(k):
+            quantised["u", k] = quantise("u", 2, u_bf[k][:])
 
-        def stage1(s):
+        def stage1(s, g):
             n = s // STEPS_PER_SAMPLE
-            for g in range(GROUPS):
-                tile = bank("t%d" % ((GROUPS * s + g) % 3), [P, PACK, CH], F32)
-                for t in range(PACK):
-                    cols = slice((g * PACK + t) * P, (g * PACK + t + 1) * P)
-                    nc.tensor.matmul_mx(out=tile[:, t, :], lhsT=codes["a", n][:, cols].bitcast(FP8X4),
-                                        lhsT_scale=scales["a", n][:, cols], rhs=codes["u", s][:].bitcast(FP8X4),
-                                        rhs_scale=scales["u", s][:], start=True, stop=True)
-                t_bank[s, g] = tile
+            tile = bank("t%d" % ((GROUPS * s + g) % 3), [P, PACK, CH], F32)
+            for t in range(PACK):
+                mx(tile[:, t, :], window(quantised["a", n, 2 * g + t // 2], (t % 2) * P, P),
+                   window(quantised["u", s // 2], (s % 2) * CH, CH), True, True)
+            t_bank[s, g] = tile
 
-        def sigmoid(s):
-            sig[s] = ring.tile([P, GROUPS, CH, PACK], F32, name="sig", tag="sig", bufs=3)
-            for g in range(GROUPS):
-                nc.scalar.activation(out=sig[s][:, g, :, :], in_=t_bank[s, g][:].rearrange("p t f -> p f t"),
-                                     func=ACT.Sigmoid)
+        def sigmoid(s, g):
+            if g == 0:
+                sig[s] = ring.tile([P, GROUPS * CH, PACK], F32, name="sig", tag="sig", bufs=3)
+            nc.scalar.activation(out=sig[s][:, g * CH:(g + 1) * CH, :], in_=t_bank[s, g][:].rearrange("p t f -> p f t"),
+                                 func=ACT.Sigmoid)
 
-        def w_chunk(s):
+        def w_cols(s, c0, c1):
             col = (s % STEPS_PER_SAMPLE) * CH
             lo = find(FIRST_RANGES, col)
-            return w_raw[lo][:, :, :, col - lo:col - lo + CH]
+            g = c0 // CH
+            return w_raw[lo][:, g, :, col - lo + c0 - g * CH:col - lo + c1 - g * CH]
+
+        def shares(s):
+            both = GROUPS * CH
+            if s % 2 == 0:
+                return (0, VW // PACK), (VW // PACK, both), TW
+            return (GW // PACK, both), (0, GW // PACK), TW + VW
+
+        def wm_view(s, c0, c1):
+            base = shares(s)[2]
+            return stage[:, base + c0 * PACK:base + c1 * PACK].rearrange("p (c t) -> p c t", t=PACK)
 
         def w_to_psum(s):
-            tile = bank("w%d" % (s % 2), [P, GROUPS, PACK, FV], BF16)
-            for g in range(GROUPS):
-                nc.tensor.matmul(out=tile[:, g, :, :], lhsT=ident16[:], rhs=w_chunk(s)[:, g, :, :FV], start=True, stop=True)
+            c0, c1 = shares(s)[0]
+            tile = bank("w%d" % (s % 2), [P, PACK, c1 - c0], BF16)
+            for lo, hi in ((c0, CH), (CH, c1)):
+                nc.tensor.matmul(out=tile[:, :, lo - c0:hi - c0], lhsT=ident16[:], rhs=w_cols(s, lo, hi), start=True, stop=True)
             w_bank[s] = tile
 
         def gate_vector(s):
-            nc.vector.tensor_tensor(out=wm_bf[:, :, :FV, :], in0=sig[s][:, :, :FV, :],
-                                    in1=w_bank[s][:].rearrange("p g t f -> p g f t"), op=ALU.mult)
+            c0, c1 = shares(s)[0]
+            nc.vector.tensor_tensor(out=wm_view(s, c0, c1), in0=sig[s][:, c0:c1, :],
+                                    in1=w_bank[s][:].rearrange("p t c -> p c t"), op=ALU.mult)
 
         def gate_gpsimd(s):
-            nc.gpsimd.tensor_tensor(out=wm_bf[:, :, FV:, :], in0=sig[s][:, :, FV:, :],
-                                    in1=w_chunk(s)[:, :, :, FV:].rearrange("p g t f -> p g f t"), op=ALU.mult)
+            c0, c1 = shares(s)[1]
+            nc.gpsimd.tensor_tensor(out=wm_view(s, c0, c1), in0=sig[s][:, c0:c1, :],
+                                    in1=w_cols(s, c0, c1).rearrange("p t c -> p c t"), op=ALU.mult)
 
-        def wm_quant(s):
-            codes["wm", s] = ring.tile([P, GROUPS * CH], U32, name="wm_codes", tag="wm_codes", bufs=3, align_bytes=64)
-            scales["wm", s] = ring.tile([P, GROUPS * CH], U8, name="wm_scales", tag="wm_scales", bufs=3, align_bytes=64)
-            nc.vector.quantize_mx(out=codes["wm", s][:].bitcast(FP8X4), scales=scales["wm", s][:],
-                                  in_=wm_bf[:].rearrange("p g f t -> p (g f t)"))
+        def turned_region(s):
+            return stage[:, 0:TW] if s % 2 == 0 else stage[:, TW + 2 * VW + GW:]
+
+        def step_quant(s, extra):
+            base = shares(s)[2]
+            wm_width = VW + GW
+            if extra is None:
+                quantised["wm", s] = window(quantise("step", 14, stage[:, base:base + wm_width]), 0, 2 * CH)
+            elif s % 2 == 0:
+                both = quantise("step", 14, stage[:, 0:TW + wm_width])
+                quantised[extra] = window(both, 0, 2 * P)
+                quantised["wm", s] = window(both, 2 * P, 2 * CH)
+            else:
+                both = quantise("step", 14, stage[:, base:])
+                quantised["wm", s] = window(both, 0, 2 * CH)
+                quantised[extra] = window(both, 2 * CH, 2 * P)
 
         def stage2(s):
             n = s // STEPS_PER_SAMPLE
             tile = bank("h%d" % (s % 2), [P, PACK, CH], F32)
             for t in range(PACK):
                 for g in range(GROUPS):
-                    cols = slice((t * GROUPS + g) * P, (t * GROUPS + g + 1) * P)
-                    wm_cols = slice(g * CH, (g + 1) * CH)
-                    nc.tensor.matmul_mx(out=tile[:, t, :], lhsT=codes["x", n][:, cols].bitcast(FP8X4),
-                                        lhsT_scale=scales["x", n][:, cols],
-                                        rhs=codes["wm", s][:, wm_cols].bitcast(FP8X4),
-                                        rhs_scale=scales["wm", s][:, wm_cols], start=(g == 0), stop=(g == GROUPS - 1))
+                    mx(tile[:, t, :], window(quantised["x", n, t], g * P, P), window(quantised["wm", s], g * CH, CH),
+                       g == 0, g == GROUPS - 1)
             h_bank[s] = tile
 
         def add_bias(s):
@@ -193,23 +223,21 @@ def tile_factorizedmultiplicativemodulationinr_x1_kernel(tc, x, a, u, w, bias, o
             nc.vector.tensor_tensor(out=z_sb[s][:], in0=h_bank[s][:],
                                     in1=bias_all[:, col:col + CH].unsqueeze(1).to_broadcast([P, PACK, CH]), op=ALU.add)
 
-        def y_view(s):
-            return y_sb[s // 2][:, :, (s % 2) * CH:(s % 2 + 1) * CH]
-
         def leaky(s):
             if s % 2 == 0:
                 y_sb[s // 2] = ring.tile([P, PACK, 2 * CH], F32, name="y_sb", tag="y_sb", bufs=4)
-            nc.vector.scalar_tensor_tensor(out=y_view(s), in0=z_sb[s][:], scalar=SLOPE, in1=z_sb[s][:],
-                                           op0=ALU.mult, op1=ALU.max)
+            nc.vector.scalar_tensor_tensor(out=y_sb[s // 2][:, :, (s % 2) * CH:(s % 2 + 1) * CH], in0=z_sb[s][:],
+                                           scalar=SLOPE, in1=z_sb[s][:], op0=ALU.mult, op1=ALU.max)
 
-        def y_interleave(s):
-            y_bf[s] = ring.tile([P, CH * PACK], BF16, name="y_bf", tag="y_bf", bufs=3, align_bytes=64)
-            dst, src = interleave_views(y_bf[s][:], y_view(s))
-            nc.scalar.copy(out=dst, in_=src)
+        def y_interleave(s0, s1, on_vector):
+            off, width = (s0 % 2) * CH, (s1 - s0) * CH
+            y_bf[s0] = ring.tile([P, width * PACK], BF16, name="y_bf", tag="y_bf", bufs=3, align_bytes=64)
+            dst, src = interleave_views(y_bf[s0][:], y_sb[s0 // 2][:, :, off:off + width])
+            copy_on(on_vector, dst, src)
 
-        def y_quant(s):
-            cols = slice(s * CH, (s + 1) * CH)
-            nc.vector.quantize_mx(out=out_words[:, cols].bitcast(FP8X4), scales=out_scales[:, cols], in_=y_bf[s][:])
+        def y_quant(s0, s1):
+            cols = slice(s0 * CH, s1 * CH)
+            nc.vector.quantize_mx(out=out_words[:, cols].bitcast(FP8X4), scales=out_scales[:, cols], in_=y_bf[s0][:])
 
         def store_y(s0, s1):
             n, col = s0 // STEPS_PER_SAMPLE, (s0 % STEPS_PER_SAMPLE) * CH
@@ -229,112 +257,153 @@ def tile_factorizedmultiplicativemodulationinr_x1_kernel(tc, x, a, u, w, bias, o
                 queues[q].dma_start(out=out_2[0, 4 * q:4 * q + 4, cols].bitcast(I32),
                                     in_=out_scales[32 * q:32 * q + 4, cols].bitcast(I32))
 
-        load_a(0, 0)
-        load_u(0, 0)
-        load_a(0, 1)
-        load_w(0)
-        load_u(0, 1)
-        load_x(0, 0, 2)
-        load_x(0, 2, 4)
         make_identity(nc, ident32[:])
         make_identity(nc, ident16[:])
         nc.gpsimd.memset(ones16[:], 1.0)
-        nc.gpsimd.memset(bias_row[:], 0.0)
+        nc.vector.memset(bias_row[:], 0.0)
         nc.vector.memset(warm[:], 0.0)
         nc.scalar.activation(out=warm[:], in_=warm[:], func=ACT.Sigmoid)
+        load_a(0, 0, 1)
+        load_a(0, 1, 2)
+        load_u(0, 0)
+        load_a(0, 2, 3)
+        load_a(0, 3, 4)
         nc.sync.dma_start(out=bias_row[0:1, :], in_=bias.unsqueeze(0))
-        load_a(1, 0)
-        load_w(1)
+        load_w(0)
+        load_u(0, 1)
+        load_x(0, 0, 2)
         load_u(0, 2)
-        load_a(1, 1)
+        load_w(1)
+        load_a(1, 0, 2)
+        load_x(0, 2, 4)
+        load_u(0, 3)
         load_w(2)
+        load_a(1, 2, 4)
+        load_u(1, 0)
+        load_w(3)
+        load_x(1, 0, 2)
+        load_x(1, 2, 4)
+        load_u(1, 1)
 
         turn("a", 0, 0, "turn")
         turn("a", 0, 1, "h0")
         turn("a", 0, 2, "h1")
         turn("a", 0, 3, "w1")
+        first_out("a", 0, False)
+        first_out("a", 1, False)
         u_interleave(0, True)
-        turn_out("a", 0, 0, False)
-        turn_out("a", 0, 1, True)
+        first_quant("a", 0)
         u_quant(0)
-        turn_quant("a", 0, 0)
-        turn_out("a", 0, 2, False)
-        turn_quant("a", 0, 1)
-        turn_out("a", 0, 3, True)
-        u_interleave(1, False)
-        turn_quant("a", 0, 2)
+        first_quant("a", 1)
+        stage1(0, 0)
+        first_out("a", 2, False)
+        first_out("a", 3, True)
+        first_quant("a", 2)
+        spread = bank("turn", [P, F], BF16)
+        for half in range(2):
+            cols = slice(half * 512, (half + 1) * 512)
+            nc.tensor.matmul(out=spread[:, cols], lhsT=ones16[:], rhs=bias_row[:, cols], start=True, stop=True)
+        sigmoid(0, 0)
+        nc.scalar.copy(out=bias_all[:], in_=spread[:])
+        first_quant("a", 3)
+        w_to_psum(0)
+        stage1(0, 1)
+        stage1(1, 0)
+        u_interleave(1, True)
+        sigmoid(0, 1)
+        stage1(1, 1)
         u_quant(1)
-        turn_quant("a", 0, 3)
 
-        turns = {-1: [("x", 0, 0, "turn"), ("x", 0, 1, "h0")], 0: [("x", 0, 2, "h1"), ("x", 0, 3, "turn")]}
+        turns = {}
         for n in range(1, N):
             for j in range(4):
-                turns[STEPS_PER_SAMPLE * (n - 1) + 1 + j] = [("a", n, j, "turn")]
-                turns[STEPS_PER_SAMPLE * (n - 1) + 5 + j] = [("x", n, j, "turn")]
+                turns[STEPS_PER_SAMPLE * (n - 1) + 1 + j] = ("a", n, j)
+                turns[STEPS_PER_SAMPLE * (n - 1) + 5 + j] = ("x", n, j)
 
         def live(s):
             return 0 <= s < STEPS
 
-        for s in range(-2, STEPS + 5):
-            early = s < 3
-            if live(s - 2):
-                stage2(s - 2)
+        for s in range(STEPS):
             if live(s + 1):
                 w_to_psum(s + 1)
-                sigmoid(s + 1)
-            if live(s):
-                gate_gpsimd(s)
             if live(s - 3):
-                add_bias(s - 3)
-            if live(s):
-                gate_vector(s)
-            if s == 1:
-                spread = bank("h1", [P, F], BF16)
-                for half in range(2):
-                    cols = slice(half * 512, (half + 1) * 512)
-                    nc.tensor.matmul(out=spread[:, cols], lhsT=ones16[:], rhs=bias_row[:, cols], start=True, stop=True)
-            for kind, n, j, tag in turns.get(s, []):
-                turn(kind, n, j, tag)
-            if live(s + 2):
-                stage1(s + 2)
-            if live(s + 4):
-                u_interleave(s + 4, False)
-            for kind, n, j, tag in turns.get(s, []):
-                turn_out(kind, n, j, early)
-            if s == 1:
-                nc.scalar.copy(out=bias_all[:], in_=spread[:])
-            if live(s - 3):
-                leaky(s - 3)
-            for kind, n, j, tag in turns.get(s - 1, []):
-                turn_quant(kind, n, j)
-            if live(s + 3) and s + 3 >= 2:
-                u_quant(s + 3)
+                stage2(s - 3)
+            if live(s + 1):
+                sigmoid(s + 1, 0)
+                sigmoid(s + 1, 1)
+            gate_gpsimd(s)
             if live(s - 4):
-                y_quant(s - 4)
-            if live(s):
-                wm_quant(s)
-            if live(s - 3):
-                y_interleave(s - 3)
+                add_bias(s - 4)
+            gate_vector(s)
+            if s in (1, 2):
+                first_out("x", 2 * s - 2, True)
+                first_out("x", 2 * s - 1, False)
+            if s in turns:
+                turn(*turns[s], "turn")
+            if live(s + 2):
+                stage1(s + 2, 0)
+                stage1(s + 2, 1)
+            if s in (0, 1):
+                turn("x", 0, 2 * s, "h0")
+                turn("x", 0, 2 * s + 1, "h1")
+            if s % 2 == 0 and live(s + 4):
+                u_interleave(s // 2 + 2, s < 3)
+            if s % 2 == 1 and live(s - 7):
+                y_interleave(s - 7, s - 5, False)
+            if s in turns:
+                turn_out(*turns[s], False, turned_region(s + 1))
+            if s % 2 == 1 and live(s + 3):
+                u_quant(s // 2 + 2)
+            if s % 2 == 0 and live(s - 8):
+                y_quant(s - 8, s - 6)
+            if s in (1, 2):
+                first_quant("x", 2 * s - 2)
+            step_quant(s, turns.get(s - 1))
+            if s in (1, 2):
+                first_quant("x", 2 * s - 1)
+            if live(s - 4):
+                leaky(s - 4)
 
-            done = s - 3
-            if live(done) and done >= STEPS - 2:
-                store_y(done, done + 1)
-            elif live(done) and done % 2 == 1:
-                store_y(done - 1, done + 1)
-            packed = s - 4
-            if packed == STEPS - 2:
-                store_words(STEPS - 4, STEPS - 1)
-                store_scales(0, STEPS - 1, [nc.sync] * 4)
-            elif packed == STEPS - 1:
-                store_words(STEPS - 1, STEPS)
-                store_scales(STEPS - 1, STEPS, [nc.sync, nc.scalar, nc.sync, nc.scalar])
-            elif live(packed) and packed % 4 == 3:
-                store_words(packed - 3, packed + 1)
+            if s % 2 == 1 and live(s - 5):
+                store_y(s - 5, s - 3)
+            if s % 4 == 2 and live(s - 10):
+                store_words(s - 10, s - 6)
 
-            ahead, phase = s // STEPS_PER_SAMPLE + 1, s % STEPS_PER_SAMPLE
-            if 1 <= ahead < N and phase == 0:
+            ahead, phase = s // STEPS_PER_SAMPLE + 2, s % STEPS_PER_SAMPLE
+            if ahead < N and phase == 5:
+                load_a(ahead, 0, 2)
+                load_a(ahead, 2, 4)
+            if ahead < N and phase == 7:
                 load_u(ahead, 0)
-                load_x(ahead, 0, PACK)
-            if 1 <= ahead < N - 1 and phase == 4:
-                load_a(ahead + 1, 0)
-                load_a(ahead + 1, 1)
+                load_u(ahead, 1)
+            if 2 <= ahead - 1 < N and phase == 1:
+                load_x(ahead - 1, 0, PACK)
+
+        e = STEPS
+        store_scales(0, e - 8, [nc.sync] * 4)
+        stage2(e - 3)
+        y_interleave(e - 6, e - 4, False)
+        add_bias(e - 4)
+        stage2(e - 2)
+        y_quant(e - 8, e - 6)
+        add_bias(e - 3)
+        stage2(e - 1)
+        leaky(e - 4)
+        leaky(e - 3)
+        store_y(e - 4, e - 2)
+        y_interleave(e - 4, e - 2, False)
+        add_bias(e - 2)
+        add_bias(e - 1)
+        leaky(e - 2)
+        y_quant(e - 6, e - 4)
+        store_y(e - 2, e - 1)
+        store_words(e - 8, e - 4)
+        leaky(e - 1)
+        y_interleave(e - 2, e - 1, False)
+        y_quant(e - 4, e - 2)
+        store_y(e - 1, e)
+        y_interleave(e - 1, e, True)
+        y_quant(e - 2, e - 1)
+        y_quant(e - 1, e)
+        store_words(e - 4, e)
+        store_scales(e - 8, e, [nc.scalar, nc.sync, nc.scalar, nc.sync])

@@ -18,11 +18,16 @@ ALU = mybir.AluOpType
 P = 128
 PACK = 4
 GROUPS = D // (P * PACK)
-CH = 128
-STEPS_PER_SAMPLE = F // CH
+CH = 256
+STEPS_PER_SAMPLE = GROUPS * F // CH
 STEPS = N * STEPS_PER_SAMPLE
 GW = 320
-VW = GROUPS * CH * PACK - GW
+VW = CH * PACK - GW
+T_BANKS = 3
+RUN = 1
+T_LAST = 0
+U_VECTOR = 48
+OUT_FIRST = 0
 TW = 2 * P * PACK
 SLOPE = 0.2
 FIRST_RANGES = [(0, 256), (256, 512), (512, 768), (768, 1024)]
@@ -79,11 +84,10 @@ def tile_factorizedmultiplicativemodulationinr_x1_kernel(tc, x, a, u, w, bias, o
             view = u[n].rearrange("(p j) f -> p j f", j=PACK)
             nc.sync.dma_start(out=u_raw[n, lo][:], in_=view[:, :, lo:hi])
 
-        def load_w(i):
+        def load_w(i, g):
             lo, hi = FIRST_RANGES[i]
-            for g in range(GROUPS):
-                view = w[g * P * PACK:(g + 1) * P * PACK, :].rearrange("(p t) f -> p t f", t=PACK)
-                nc.sync.dma_start(out=w_raw[lo][:, g, :, :], in_=view[:, :, lo:hi])
+            view = w[g * P * PACK:(g + 1) * P * PACK, :].rearrange("(p t) f -> p t f", t=PACK)
+            nc.sync.dma_start(out=w_raw[lo][:, g, :, :], in_=view[:, :, lo:hi])
 
         turned, grouped, quantised = {}, {}, {}
 
@@ -134,62 +138,64 @@ def tile_factorizedmultiplicativemodulationinr_x1_kernel(tc, x, a, u, w, bias, o
         def interleave_views(dst, src):
             return (dst.rearrange("p (c i t) -> p c t i", i=4, t=PACK), src.rearrange("p t (c i) -> p c t i", i=4))
 
-        def u_interleave(k, on_vector):
-            n, col = 2 * k // STEPS_PER_SAMPLE, (2 * k % STEPS_PER_SAMPLE) * CH
+        def first_col(s):
+            return (s % STEPS_PER_SAMPLE) // GROUPS * CH
+
+        def u_interleave(k, c0, c1, on_vector):
+            n, col = 2 * k // STEPS_PER_SAMPLE, first_col(2 * k)
             lo = find(u_ranges[n], col)
-            u_bf[k] = ring.tile([P, 2 * CH * PACK], BF16, name="u_bf", tag="u_bf", align_bytes=64)
-            dst, src = interleave_views(u_bf[k][:], u_raw[n, lo][:, :, col - lo:col - lo + 2 * CH])
+            if k not in u_bf:
+                u_bf[k] = ring.tile([P, CH * PACK], BF16, name="u_bf", tag="u_bf", align_bytes=64)
+            dst, src = interleave_views(u_bf[k][:, c0 * PACK:c1 * PACK], u_raw[n, lo][:, :, col - lo + c0:col - lo + c1])
             copy_on(on_vector, dst, src)
 
         def u_quant(k):
-            quantised["u", k] = quantise("u", 2, u_bf[k][:])
+            quantised["u", k] = window(quantise("u", 2, u_bf[k][:]), 0, CH)
 
-        def stage1(s, g):
-            n = s // STEPS_PER_SAMPLE
-            tile = bank("t%d" % ((GROUPS * s + g) % 3), [P, PACK, CH], F32)
+        def stage1(s, h):
+            n, g = s // STEPS_PER_SAMPLE, s % GROUPS
+            tile = bank("t%d" % ((2 * s + h) % T_BANKS), [P, PACK, P], F32)
             for t in range(PACK):
                 mx(tile[:, t, :], window(quantised["a", n, 2 * g + t // 2], (t % 2) * P, P),
-                   window(quantised["u", s // 2], (s % 2) * CH, CH), True, True)
-            t_bank[s, g] = tile
+                   window(quantised["u", s // 2], h * P, P), True, True)
+            t_bank[s, h] = tile
 
-        def sigmoid(s, g):
-            if g == 0:
-                sig[s] = ring.tile([P, GROUPS * CH, PACK], F32, name="sig", tag="sig", bufs=3)
-            nc.scalar.activation(out=sig[s][:, g * CH:(g + 1) * CH, :], in_=t_bank[s, g][:].rearrange("p t f -> p f t"),
+        def sigmoid(s, h):
+            if h == 0:
+                sig[s] = ring.tile([P, CH, PACK], F32, name="sig", tag="sig", bufs=3)
+            nc.scalar.activation(out=sig[s][:, h * P:(h + 1) * P, :], in_=t_bank[s, h][:].rearrange("p t f -> p f t"),
                                  func=ACT.Sigmoid)
 
         def w_cols(s, c0, c1):
-            col = (s % STEPS_PER_SAMPLE) * CH
+            col = first_col(s)
             lo = find(FIRST_RANGES, col)
-            g = c0 // CH
-            return w_raw[lo][:, g, :, col - lo + c0 - g * CH:col - lo + c1 - g * CH]
+            return w_raw[lo][:, s % GROUPS, :, col - lo + c0:col - lo + c1]
 
         def shares(s):
-            both = GROUPS * CH
             if s % 2 == 0:
-                return (0, VW // PACK), (VW // PACK, both), TW
-            return (GW // PACK, both), (0, GW // PACK), TW + VW
+                return (0, VW // PACK), (VW // PACK, CH), TW
+            return (GW // PACK, CH), (0, GW // PACK), TW + VW
 
-        def wm_view(s, c0, c1):
+        def gate(engine, s, c0, c1, w_view):
             base = shares(s)[2]
-            return stage[:, base + c0 * PACK:base + c1 * PACK].rearrange("p (c t) -> p c t", t=PACK)
+            engine.tensor_tensor(out=stage[:, base + c0 * PACK:base + c1 * PACK].rearrange("p (c t) -> p c t", t=PACK),
+                                 in0=sig[s][:, c0:c1, :], in1=w_view.rearrange("p t c -> p c t"), op=ALU.mult)
 
         def w_to_psum(s):
             c0, c1 = shares(s)[0]
             tile = bank("w%d" % (s % 2), [P, PACK, c1 - c0], BF16)
-            for lo, hi in ((c0, CH), (CH, c1)):
-                nc.tensor.matmul(out=tile[:, :, lo - c0:hi - c0], lhsT=ident16[:], rhs=w_cols(s, lo, hi), start=True, stop=True)
+            for h in range(2):
+                nc.tensor.matmul(out=tile[:, 2 * h:2 * h + 2, :], lhsT=ident16[:], rhs=w_cols(s, c0, c1)[:, 2 * h:2 * h + 2, :],
+                                 start=True, stop=True)
             w_bank[s] = tile
 
         def gate_vector(s):
             c0, c1 = shares(s)[0]
-            nc.vector.tensor_tensor(out=wm_view(s, c0, c1), in0=sig[s][:, c0:c1, :],
-                                    in1=w_bank[s][:].rearrange("p t c -> p c t"), op=ALU.mult)
+            gate(nc.vector, s, c0, c1, w_bank[s][:])
 
         def gate_gpsimd(s):
             c0, c1 = shares(s)[1]
-            nc.gpsimd.tensor_tensor(out=wm_view(s, c0, c1), in0=sig[s][:, c0:c1, :],
-                                    in1=w_cols(s, c0, c1).rearrange("p t c -> p c t"), op=ALU.mult)
+            gate(nc.gpsimd, s, c0, c1, w_cols(s, c0, c1))
 
         def turned_region(s):
             return stage[:, 0:TW] if s % 2 == 0 else stage[:, TW + 2 * VW + GW:]
@@ -198,57 +204,55 @@ def tile_factorizedmultiplicativemodulationinr_x1_kernel(tc, x, a, u, w, bias, o
             base = shares(s)[2]
             wm_width = VW + GW
             if extra is None:
-                quantised["wm", s] = window(quantise("step", 14, stage[:, base:base + wm_width]), 0, 2 * CH)
+                quantised["wm", s] = window(quantise("step", 14, stage[:, base:base + wm_width]), 0, CH)
             elif s % 2 == 0:
                 both = quantise("step", 14, stage[:, 0:TW + wm_width])
                 quantised[extra] = window(both, 0, 2 * P)
-                quantised["wm", s] = window(both, 2 * P, 2 * CH)
+                quantised["wm", s] = window(both, 2 * P, CH)
             else:
                 both = quantise("step", 14, stage[:, base:])
-                quantised["wm", s] = window(both, 0, 2 * CH)
-                quantised[extra] = window(both, 2 * CH, 2 * P)
+                quantised["wm", s] = window(both, 0, CH)
+                quantised[extra] = window(both, CH, 2 * P)
 
-        def stage2(s):
-            n = s // STEPS_PER_SAMPLE
-            tile = bank("h%d" % (s % 2), [P, PACK, CH], F32)
-            for t in range(PACK):
+        def stage2(e):
+            n, b = e // STEPS_PER_SAMPLE, e % 2
+            tile = bank("h%d" % b, [P, 2, CH], F32)
+            for i in range(2):
                 for g in range(GROUPS):
-                    mx(tile[:, t, :], window(quantised["x", n, t], g * P, P), window(quantised["wm", s], g * CH, CH),
+                    mx(tile[:, i, :], window(quantised["x", n, 2 * b + i], g * P, P), quantised["wm", e - b + g],
                        g == 0, g == GROUPS - 1)
-            h_bank[s] = tile
+            h_bank[e] = tile
 
-        def add_bias(s):
-            col = (s % STEPS_PER_SAMPLE) * CH
-            z_sb[s] = ring.tile([P, PACK, CH], F32, name="z_sb", tag="z_sb")
-            nc.vector.tensor_tensor(out=z_sb[s][:], in0=h_bank[s][:],
-                                    in1=bias_all[:, col:col + CH].unsqueeze(1).to_broadcast([P, PACK, CH]), op=ALU.add)
+        def add_bias(e):
+            col = first_col(e)
+            z_sb[e] = ring.tile([P, 2, CH], F32, name="z_sb", tag="z_sb")
+            nc.vector.tensor_tensor(out=z_sb[e][:], in0=h_bank[e][:],
+                                    in1=bias_all[:, col:col + CH].unsqueeze(1).to_broadcast([P, 2, CH]), op=ALU.add)
 
-        def leaky(s):
-            if s % 2 == 0:
-                y_sb[s // 2] = ring.tile([P, PACK, 2 * CH], F32, name="y_sb", tag="y_sb", bufs=4)
-            nc.vector.scalar_tensor_tensor(out=y_sb[s // 2][:, :, (s % 2) * CH:(s % 2 + 1) * CH], in0=z_sb[s][:],
-                                           scalar=SLOPE, in1=z_sb[s][:], op0=ALU.mult, op1=ALU.max)
+        def leaky(e, c0, c1):
+            if e % 2 == 0 and c0 == 0:
+                y_sb[e // 2] = ring.tile([P, PACK, CH], F32, name="y_sb", tag="y_sb", bufs=4)
+            b = e % 2
+            nc.vector.scalar_tensor_tensor(out=y_sb[e // 2][:, 2 * b:2 * b + 2, c0:c1], in0=z_sb[e][:, :, c0:c1],
+                                           scalar=SLOPE, in1=z_sb[e][:, :, c0:c1], op0=ALU.mult, op1=ALU.max)
 
-        def y_interleave(s0, s1, on_vector):
-            off, width = (s0 % 2) * CH, (s1 - s0) * CH
-            y_bf[s0] = ring.tile([P, width * PACK], BF16, name="y_bf", tag="y_bf", bufs=3, align_bytes=64)
-            dst, src = interleave_views(y_bf[s0][:], y_sb[s0 // 2][:, :, off:off + width])
+        def y_interleave(k, c0, c1, on_vector):
+            y_bf[k, c0] = ring.tile([P, (c1 - c0) * PACK], BF16, name="y_bf", tag="y_bf", bufs=3, align_bytes=64)
+            dst, src = interleave_views(y_bf[k, c0][:], y_sb[k][:, :, c0:c1])
             copy_on(on_vector, dst, src)
 
-        def y_quant(s0, s1):
-            cols = slice(s0 * CH, s1 * CH)
-            nc.vector.quantize_mx(out=out_words[:, cols].bitcast(FP8X4), scales=out_scales[:, cols], in_=y_bf[s0][:])
+        def y_quant(k, c0, c1):
+            cols = slice(k * CH + c0, k * CH + c1)
+            nc.vector.quantize_mx(out=out_words[:, cols].bitcast(FP8X4), scales=out_scales[:, cols], in_=y_bf[k, c0][:])
 
-        def store_y(s0, s1):
-            n, col = s0 // STEPS_PER_SAMPLE, (s0 % STEPS_PER_SAMPLE) * CH
-            view = out_0[n].rearrange("(p t) f -> p t f", t=PACK)
-            off = (s0 % 2) * CH
-            width = (s1 - s0) * CH
-            nc.sync.dma_start(out=view[:, :, col:col + width], in_=y_sb[s0 // 2][:, :, off:off + width])
+        def store_y(k, t0, t1):
+            col = first_col(2 * k)
+            view = out_0[2 * k // STEPS_PER_SAMPLE].rearrange("(p t) f -> p t f", t=PACK)
+            nc.sync.dma_start(out=view[:, t0:t1, col:col + CH], in_=y_sb[k][:, t0:t1, :])
 
-        def store_words(s0, s1):
+        def store_words(c0, c1):
             view = out_1[0].rearrange("p m t -> p (m t)").bitcast(I32)
-            cols = slice(s0 * CH, s1 * CH)
+            cols = slice(c0, c1)
             nc.sync.dma_start(out=view[:, cols], in_=out_words[:, cols].bitcast(I32))
 
         def store_scales(s0, s1, queues):
@@ -268,66 +272,84 @@ def tile_factorizedmultiplicativemodulationinr_x1_kernel(tc, x, a, u, w, bias, o
         load_u(0, 0)
         load_a(0, 2, 3)
         load_a(0, 3, 4)
-        nc.sync.dma_start(out=bias_row[0:1, :], in_=bias.unsqueeze(0))
-        load_w(0)
+        load_w(0, 0)
+        load_w(0, 1)
         load_u(0, 1)
+        nc.sync.dma_start(out=bias_row[0:1, :], in_=bias.unsqueeze(0))
         load_x(0, 0, 2)
+        load_w(1, 0)
+        load_w(1, 1)
         load_u(0, 2)
-        load_w(1)
-        load_a(1, 0, 2)
         load_x(0, 2, 4)
+        load_a(1, 0, 2)
         load_u(0, 3)
-        load_w(2)
+        load_w(2, 0)
+        load_w(2, 1)
         load_a(1, 2, 4)
         load_u(1, 0)
-        load_w(3)
+        load_w(3, 0)
+        load_w(3, 1)
         load_x(1, 0, 2)
         load_x(1, 2, 4)
         load_u(1, 1)
 
-        turn("a", 0, 0, "turn")
+        turn("a", 0, 0, "turn0")
         turn("a", 0, 1, "h0")
-        turn("a", 0, 2, "h1")
-        turn("a", 0, 3, "w1")
         first_out("a", 0, False)
+        u_interleave(0, 0, CH, True)
         first_out("a", 1, False)
-        u_interleave(0, True)
         first_quant("a", 0)
         u_quant(0)
         first_quant("a", 1)
+        turn("a", 0, 2, "h1")
+        turn("a", 0, 3, "w1")
         stage1(0, 0)
+        stage1(0, 1)
+        w_to_psum(0)
+        spread = bank("turn0", [P, F], BF16)
+        for part in range(2):
+            cols = slice(part * 512, (part + 1) * 512)
+            nc.tensor.matmul(out=spread[:, cols], lhsT=ones16[:], rhs=bias_row[:, cols], start=True, stop=True)
         first_out("a", 2, False)
         first_out("a", 3, True)
-        first_quant("a", 2)
-        spread = bank("turn", [P, F], BF16)
-        for half in range(2):
-            cols = slice(half * 512, (half + 1) * 512)
-            nc.tensor.matmul(out=spread[:, cols], lhsT=ones16[:], rhs=bias_row[:, cols], start=True, stop=True)
         sigmoid(0, 0)
-        nc.scalar.copy(out=bias_all[:], in_=spread[:])
-        first_quant("a", 3)
-        w_to_psum(0)
-        stage1(0, 1)
-        stage1(1, 0)
-        u_interleave(1, True)
         sigmoid(0, 1)
+        first_quant("a", 2)
+        first_quant("a", 3)
+        stage1(1, 0)
         stage1(1, 1)
+        w_to_psum(1)
+        u_interleave(1, 0, CH, True)
+        gate_gpsimd(0)
+        gate_vector(0)
+        nc.vector.tensor_copy(out=bias_all[:], in_=spread[:])
         u_quant(1)
+        step_quant(0, None)
+        sigmoid(1, 0)
+        sigmoid(1, 1)
+        turn("x", 0, 0, "h0")
+        turn("x", 0, 1, "h1")
+        stage1(2, 0)
+        stage1(2, 1)
+        u_interleave(2, 0, CH, False)
 
-        turns = {}
+        turns, outs = {}, {}
         for n in range(1, N):
-            for j in range(4):
-                turns[STEPS_PER_SAMPLE * (n - 1) + 1 + j] = ("a", n, j)
-                turns[STEPS_PER_SAMPLE * (n - 1) + 5 + j] = ("x", n, j)
+            for i, kind in enumerate("aaaaxxxx"):
+                leaves = STEPS_PER_SAMPLE * (n - 1) + 2 + i
+                outs[leaves] = (kind, n, i % 4)
+                turns.setdefault(leaves - i % RUN - T_LAST, []).append((kind, n, i % 4, "turn%d" % (i % RUN)))
 
         def live(s):
             return 0 <= s < STEPS
 
-        for s in range(STEPS):
+        for s in range(1, STEPS):
             if live(s + 1):
                 w_to_psum(s + 1)
             if live(s - 3):
                 stage2(s - 3)
+            if s in outs and OUT_FIRST:
+                turn_out(*outs[s], False, turned_region(s + 1))
             if live(s + 1):
                 sigmoid(s + 1, 0)
                 sigmoid(s + 1, 1)
@@ -335,39 +357,46 @@ def tile_factorizedmultiplicativemodulationinr_x1_kernel(tc, x, a, u, w, bias, o
             if live(s - 4):
                 add_bias(s - 4)
             gate_vector(s)
-            if s in (1, 2):
-                first_out("x", 2 * s - 2, True)
-                first_out("x", 2 * s - 1, False)
-            if s in turns:
-                turn(*turns[s], "turn")
+            for j in {1: (0, 1), 2: (2,), 3: (3,)}.get(s, ()):
+                first_out("x", j, True)
+            if not T_LAST:
+                for args in turns.get(s, []):
+                    turn(*args)
             if live(s + 2):
                 stage1(s + 2, 0)
                 stage1(s + 2, 1)
-            if s in (0, 1):
-                turn("x", 0, 2 * s, "h0")
-                turn("x", 0, 2 * s + 1, "h1")
+            if s == 1:
+                turn("x", 0, 2, "h0")
+                turn("x", 0, 3, "h1")
             if s % 2 == 0 and live(s + 4):
-                u_interleave(s // 2 + 2, s < 3)
+                split = U_VECTOR if s in outs and s > 3 else 0
+                if split > 0:
+                    u_interleave(s // 2 + 2, 0, split, True)
+                if split < CH:
+                    u_interleave(s // 2 + 2, split, CH, False)
             if s % 2 == 1 and live(s - 7):
-                y_interleave(s - 7, s - 5, False)
-            if s in turns:
-                turn_out(*turns[s], False, turned_region(s + 1))
+                y_interleave((s - 7) // 2, 0, CH, False)
+            if s in outs and not OUT_FIRST:
+                turn_out(*outs[s], False, turned_region(s + 1))
+            if T_LAST:
+                for args in turns.get(s, []):
+                    turn(*args)
             if s % 2 == 1 and live(s + 3):
                 u_quant(s // 2 + 2)
             if s % 2 == 0 and live(s - 8):
-                y_quant(s - 8, s - 6)
-            if s in (1, 2):
-                first_quant("x", 2 * s - 2)
-            step_quant(s, turns.get(s - 1))
-            if s in (1, 2):
-                first_quant("x", 2 * s - 1)
+                y_quant((s - 8) // 2, 0, CH)
+            if s in (1, 2, 3):
+                first_quant("x", (0, 2, 3)[s - 1])
+            step_quant(s, outs.get(s - 1))
+            if s == 1:
+                first_quant("x", 1)
             if live(s - 4):
-                leaky(s - 4)
+                leaky(s - 4, 0, CH)
 
             if s % 2 == 1 and live(s - 5):
-                store_y(s - 5, s - 3)
+                store_y((s - 5) // 2, 0, PACK)
             if s % 4 == 2 and live(s - 10):
-                store_words(s - 10, s - 6)
+                store_words((s - 10) // 2 * CH, (s - 6) // 2 * CH)
 
             ahead, phase = s // STEPS_PER_SAMPLE + 2, s % STEPS_PER_SAMPLE
             if ahead < N and phase == 5:
@@ -376,34 +405,36 @@ def tile_factorizedmultiplicativemodulationinr_x1_kernel(tc, x, a, u, w, bias, o
             if ahead < N and phase == 7:
                 load_u(ahead, 0)
                 load_u(ahead, 1)
-            if 2 <= ahead - 1 < N and phase == 1:
+            if 2 <= ahead - 1 < N and phase == 2:
                 load_x(ahead - 1, 0, PACK)
 
-        e = STEPS
-        store_scales(0, e - 8, [nc.sync] * 4)
+        e, k, half = STEPS, STEPS // 2, CH // 2
+        store_scales(0, k - 4, [nc.sync] * 4)
         stage2(e - 3)
-        y_interleave(e - 6, e - 4, False)
+        y_interleave(k - 3, 0, CH, False)
         add_bias(e - 4)
         stage2(e - 2)
-        y_quant(e - 8, e - 6)
+        y_quant(k - 4, 0, CH)
         add_bias(e - 3)
         stage2(e - 1)
-        leaky(e - 4)
-        leaky(e - 3)
-        store_y(e - 4, e - 2)
-        y_interleave(e - 4, e - 2, False)
+        leaky(e - 4, 0, CH)
+        leaky(e - 3, 0, CH)
+        store_y(k - 2, 0, PACK)
+        y_interleave(k - 2, 0, CH, False)
         add_bias(e - 2)
         add_bias(e - 1)
-        leaky(e - 2)
-        y_quant(e - 6, e - 4)
-        store_y(e - 2, e - 1)
-        store_words(e - 8, e - 4)
-        leaky(e - 1)
-        y_interleave(e - 2, e - 1, False)
-        y_quant(e - 4, e - 2)
-        store_y(e - 1, e)
-        y_interleave(e - 1, e, True)
-        y_quant(e - 2, e - 1)
-        y_quant(e - 1, e)
-        store_words(e - 4, e)
-        store_scales(e - 8, e, [nc.scalar, nc.sync, nc.scalar, nc.sync])
+        leaky(e - 2, 0, CH)
+        store_y(k - 1, 0, 2)
+        leaky(e - 1, 0, half)
+        y_interleave(k - 1, 0, half, False)
+        y_quant(k - 3, 0, CH)
+        store_words((k - 4) * CH, (k - 2) * CH)
+        leaky(e - 1, half, CH)
+        store_y(k - 1, 2, PACK)
+        y_quant(k - 2, 0, CH)
+        y_interleave(k - 1, half, CH, True)
+        y_quant(k - 1, 0, half)
+        store_words((k - 2) * CH, k * CH - half)
+        y_quant(k - 1, half, CH)
+        store_words(k * CH - half, k * CH)
+        store_scales(k - 4, k, [nc.scalar, nc.sync, nc.scalar, nc.sync])

@@ -26,7 +26,7 @@ VW = CH * PACK - GW
 T_BANKS = 3
 RUN = 1
 T_LAST = 0
-U_VECTOR = 48
+U_VECTOR = 32
 OUT_FIRST = 0
 TW = 2 * P * PACK
 SLOPE = 0.2
@@ -434,7 +434,6 @@ def tile_factorizedmultiplicativemodulationinr_x1_kernel(tc, x, a, u, w, bias, o
         y_quant(k - 2, 0, CH)
         y_interleave(k - 1, half, CH, True)
         y_quant(k - 1, 0, half)
-        store_words((k - 2) * CH, k * CH - half)
         y_quant(k - 1, half, CH)
-        store_words(k * CH - half, k * CH)
+        store_words((k - 2) * CH, k * CH)
         store_scales(k - 4, k, [nc.scalar, nc.sync, nc.scalar, nc.sync])

from contextlib import ExitStack

import concourse.mybir as mybir
from concourse.masks import make_identity

N, TOK, D, R, F = 4, 512, 1024, 512, 1024
FLOPS = N * (2 * D * R * F + 2 * TOK * D * F)

F32 = mybir.dt.float32
BF16 = mybir.dt.bfloat16
I32 = mybir.dt.int32
U32 = mybir.dt.uint32
U8 = mybir.dt.uint8
FP8X4 = mybir.dt.float8_e4m3fn_x4
ACT = mybir.ActivationFunctionType
ALU = mybir.AluOpType

P = 128
PACK = 4
GROUPS = D // (P * PACK)
CH = 256
STEPS_PER_SAMPLE = GROUPS * F // CH
STEPS = N * STEPS_PER_SAMPLE
GW = 320
VW = CH * PACK - GW
T_BANKS = 3
RUN = 1
T_LAST = 0
U_VECTOR = 32
OUT_FIRST = 0
TW = 2 * P * PACK
SLOPE = 0.2
FIRST_RANGES = [(0, 256), (256, 512), (512, 768), (768, 1024)]


def tile_factorizedmultiplicativemodulationinr_x1_kernel(tc, x, a, u, w, bias, out_0, out_1, out_2):
    nc = tc.nc
    with ExitStack() as ctx:
        keep = ctx.enter_context(tc.tile_pool(name="keep", bufs=1))
        ring = ctx.enter_context(tc.tile_pool(name="ring", bufs=2))
        psum = ctx.enter_context(tc.psum_pool(name="psum", bufs=1))
        ctx.enter_context(tc.manual_schedule())

        def bank(tag, shape, dtype):
            return psum.tile(shape, dtype, name=tag, tag=tag)

        ident32 = keep.tile([P, P], F32, name="ident32")
        ident16 = keep.tile([P, P], BF16, name="ident16")
        ones16 = keep.tile([P, P], BF16, name="ones16")
        bias_row = keep.tile([P, F], BF16, name="bias_row")
        bias_all = keep.tile([P, F], BF16, name="bias_all")
        warm = keep.tile([P, 1], F32, name="warm")
        stage = keep.tile([P, 2 * TW + 2 * VW + GW], BF16, name="stage", align_bytes=64)
        out_words = keep.tile([P, N * F], U32, name="out_words", align_bytes=64)
        out_scales = keep.tile([P, N * F], U8, name="out_scales", align_bytes=64)
        u_ranges = [FIRST_RANGES] + [[(0, F // 2), (F // 2, F)]] * (N - 1)
        a_raw, x_raw, u_raw = {}, {}, {}
        for lo, hi in FIRST_RANGES:
            u_raw[0, lo] = keep.tile([P, PACK, hi - lo], BF16, name="u_first%d" % lo)
        w_raw = {}
        for lo, hi in FIRST_RANGES:
            w_raw[lo] = keep.tile([P, GROUPS, PACK, hi - lo], BF16, name="w_raw%d" % lo)

        def find(ranges, col):
            return [lo for lo, hi in ranges if lo <= col < hi][0]

        def load_a(n, j0, j1):
            if j0 == 0:
                a_raw[n] = ring.tile([P, GROUPS * PACK * R], BF16, name="a_raw", tag="a_raw")
            g, t0, t1 = j0 // 2, 2 * (j0 % 2), 2 * (j0 % 2) + 2 * (j1 - j0)
            rows = a[n, g * P * PACK:(g + 1) * P * PACK, :].rearrange("(m t) r -> m (t r)", t=PACK)
            nc.sync.dma_start(out=a_raw[n][:, 2 * j0 * R:2 * j1 * R], in_=rows[:, t0 * R:t1 * R])

        def load_x(n, t0, t1):
            if t0 == 0:
                x_raw[n] = ring.tile([P, PACK, D], BF16, name="x_raw", tag="x_raw")
            view = x[n].rearrange("(m t) d -> m t d", t=PACK)
            nc.sync.dma_start(out=x_raw[n][:, t0:t1, :], in_=view[:, t0:t1, :])

        def load_u(n, i):
            lo, hi = u_ranges[n][i]
            if n > 0:
                u_raw[n, lo] = ring.tile([P, PACK, hi - lo], BF16, name="u_raw", tag="u_raw", bufs=4)
            view = u[n].rearrange("(p j) f -> p j f", j=PACK)
            nc.sync.dma_start(out=u_raw[n, lo][:], in_=view[:, :, lo:hi])

        def load_w(i, g):
            lo, hi = FIRST_RANGES[i]
            view = w[g * P * PACK:(g + 1) * P * PACK, :].rearrange("(p t) f -> p t f", t=PACK)
            nc.sync.dma_start(out=w_raw[lo][:, g, :, :], in_=view[:, :, lo:hi])

        turned, grouped, quantised = {}, {}, {}

        def copy_on(on_vector, dst, src):
            if on_vector:
                nc.vector.tensor_copy(out=dst, in_=src)
            else:
                nc.scalar.copy(out=dst, in_=src)

        def quantise(tag, bufs, src):
            width = src.shape[1] // PACK
            codes = ring.tile([P, width], U32, name=tag + "_codes", tag=tag + "_codes", bufs=bufs, align_bytes=64)
            scales = ring.tile([P, width], U8, name=tag + "_scales", tag=tag + "_scales", bufs=bufs, align_bytes=64)
            nc.vector.quantize_mx(out=codes[:].bitcast(FP8X4), scales=scales[:], in_=src)
            return codes, scales

        def window(pair, col, width):
            return pair[0][:, col:col + width], pair[1][:, col:col + width]

        def mx(out, lhs, rhs, start, stop):
            nc.tensor.matmul_mx(out=out, lhsT=lhs[0].bitcast(FP8X4), lhsT_scale=lhs[1], rhs=rhs[0].bitcast(FP8X4),
                                rhs_scale=rhs[1], start=start, stop=stop)

        def turn(kind, n, j, tag):
            tile = bank(tag, [P, 2, 2, P], F32)
            for i in range(2):
                if kind == "a":
                    words = a_raw[n][:, (2 * j + i) * R:(2 * j + i + 1) * R].bitcast(F32)
                else:
                    words = x_raw[n][:, j, i * P * PACK:(i + 1) * P * PACK].bitcast(F32)
                for half in range(2):
                    nc.tensor.transpose(tile[:, i, half, :], words[:, half:2 * P:2], ident32[:])
            turned[kind, n, j] = tile

        def turn_out(kind, n, j, on_vector, dst):
            copy_on(on_vector, dst.bitcast(F32).rearrange("p (i m h) -> p i m h", i=2, h=2),
                    turned[kind, n, j][:].rearrange("p i h m -> p i m h"))

        def first_out(kind, j, on_vector):
            grouped[kind, j] = ring.tile([P, TW], BF16, name="grouped", tag="grouped", bufs=4, align_bytes=64)
            turn_out(kind, 0, j, on_vector, grouped[kind, j][:])

        def first_quant(kind, j):
            quantised[kind, 0, j] = window(quantise("first", 8, grouped[kind, j][:]), 0, 2 * P)

        u_bf, t_bank, sig, w_bank, h_bank, z_sb, y_sb, y_bf = {}, {}, {}, {}, {}, {}, {}, {}

        def interleave_views(dst, src):
            return (dst.rearrange("p (c i t) -> p c t i", i=4, t=PACK), src.rearrange("p t (c i) -> p c t i", i=4))

        def first_col(s):
            return (s % STEPS_PER_SAMPLE) // GROUPS * CH

        def u_interleave(k, c0, c1, on_vector):
            n, col = 2 * k // STEPS_PER_SAMPLE, first_col(2 * k)
            lo = find(u_ranges[n], col)
            if k not in u_bf:
                u_bf[k] = ring.tile([P, CH * PACK], BF16, name="u_bf", tag="u_bf", align_bytes=64)
            dst, src = interleave_views(u_bf[k][:, c0 * PACK:c1 * PACK], u_raw[n, lo][:, :, col - lo + c0:col - lo + c1])
            copy_on(on_vector, dst, src)

        def u_quant(k):
            quantised["u", k] = window(quantise("u", 2, u_bf[k][:]), 0, CH)

        def stage1(s, h):
            n, g = s // STEPS_PER_SAMPLE, s % GROUPS
            tile = bank("t%d" % ((2 * s + h) % T_BANKS), [P, PACK, P], F32)
            for t in range(PACK):
                mx(tile[:, t, :], window(quantised["a", n, 2 * g + t // 2], (t % 2) * P, P),
                   window(quantised["u", s // 2], h * P, P), True, True)
            t_bank[s, h] = tile

        def sigmoid(s, h):
            if h == 0:
                sig[s] = ring.tile([P, CH, PACK], F32, name="sig", tag="sig", bufs=3)
            nc.scalar.activation(out=sig[s][:, h * P:(h + 1) * P, :], in_=t_bank[s, h][:].rearrange("p t f -> p f t"),
                                 func=ACT.Sigmoid)

        def w_cols(s, c0, c1):
            col = first_col(s)
            lo = find(FIRST_RANGES, col)
            return w_raw[lo][:, s % GROUPS, :, col - lo + c0:col - lo + c1]

        def shares(s):
            if s % 2 == 0:
                return (0, VW // PACK), (VW // PACK, CH), TW
            return (GW // PACK, CH), (0, GW // PACK), TW + VW

        def gate(engine, s, c0, c1, w_view):
            base = shares(s)[2]
            engine.tensor_tensor(out=stage[:, base + c0 * PACK:base + c1 * PACK].rearrange("p (c t) -> p c t", t=PACK),
                                 in0=sig[s][:, c0:c1, :], in1=w_view.rearrange("p t c -> p c t"), op=ALU.mult)

        def w_to_psum(s):
            c0, c1 = shares(s)[0]
            tile = bank("w%d" % (s % 2), [P, PACK, c1 - c0], BF16)
            for h in range(2):
                nc.tensor.matmul(out=tile[:, 2 * h:2 * h + 2, :], lhsT=ident16[:], rhs=w_cols(s, c0, c1)[:, 2 * h:2 * h + 2, :],
                                 start=True, stop=True)
            w_bank[s] = tile

        def gate_vector(s):
            c0, c1 = shares(s)[0]
            gate(nc.vector, s, c0, c1, w_bank[s][:])

        def gate_gpsimd(s):
            c0, c1 = shares(s)[1]
            gate(nc.gpsimd, s, c0, c1, w_cols(s, c0, c1))

        def turned_region(s):
            return stage[:, 0:TW] if s % 2 == 0 else stage[:, TW + 2 * VW + GW:]

        def step_quant(s, extra):
            base = shares(s)[2]
            wm_width = VW + GW
            if extra is None:
                quantised["wm", s] = window(quantise("step", 14, stage[:, base:base + wm_width]), 0, CH)
            elif s % 2 == 0:
                both = quantise("step", 14, stage[:, 0:TW + wm_width])
                quantised[extra] = window(both, 0, 2 * P)
                quantised["wm", s] = window(both, 2 * P, CH)
            else:
                both = quantise("step", 14, stage[:, base:])
                quantised["wm", s] = window(both, 0, CH)
                quantised[extra] = window(both, CH, 2 * P)

        def stage2(e):
            n, b = e // STEPS_PER_SAMPLE, e % 2
            tile = bank("h%d" % b, [P, 2, CH], F32)
            for i in range(2):
                for g in range(GROUPS):
                    mx(tile[:, i, :], window(quantised["x", n, 2 * b + i], g * P, P), quantised["wm", e - b + g],
                       g == 0, g == GROUPS - 1)
            h_bank[e] = tile

        def add_bias(e):
            col = first_col(e)
            z_sb[e] = ring.tile([P, 2, CH], F32, name="z_sb", tag="z_sb")
            nc.vector.tensor_tensor(out=z_sb[e][:], in0=h_bank[e][:],
                                    in1=bias_all[:, col:col + CH].unsqueeze(1).to_broadcast([P, 2, CH]), op=ALU.add)

        def leaky(e, c0, c1):
            if e % 2 == 0 and c0 == 0:
                y_sb[e // 2] = ring.tile([P, PACK, CH], F32, name="y_sb", tag="y_sb", bufs=4)
            b = e % 2
            nc.vector.scalar_tensor_tensor(out=y_sb[e // 2][:, 2 * b:2 * b + 2, c0:c1], in0=z_sb[e][:, :, c0:c1],
                                           scalar=SLOPE, in1=z_sb[e][:, :, c0:c1], op0=ALU.mult, op1=ALU.max)

        def y_interleave(k, c0, c1, on_vector):
            y_bf[k, c0] = ring.tile([P, (c1 - c0) * PACK], BF16, name="y_bf", tag="y_bf", bufs=3, align_bytes=64)
            dst, src = interleave_views(y_bf[k, c0][:], y_sb[k][:, :, c0:c1])
            copy_on(on_vector, dst, src)

        def y_quant(k, c0, c1):
            cols = slice(k * CH + c0, k * CH + c1)
            nc.vector.quantize_mx(out=out_words[:, cols].bitcast(FP8X4), scales=out_scales[:, cols], in_=y_bf[k, c0][:])

        def store_y(k, t0, t1):
            col = first_col(2 * k)
            view = out_0[2 * k // STEPS_PER_SAMPLE].rearrange("(p t) f -> p t f", t=PACK)
            nc.sync.dma_start(out=view[:, t0:t1, col:col + CH], in_=y_sb[k][:, t0:t1, :])

        def store_words(c0, c1):
            view = out_1[0].rearrange("p m t -> p (m t)").bitcast(I32)
            cols = slice(c0, c1)
            nc.sync.dma_start(out=view[:, cols], in_=out_words[:, cols].bitcast(I32))

        def store_scales(s0, s1, queues):
            cols = slice(s0 * CH, s1 * CH)
            for q in range(4):
                queues[q].dma_start(out=out_2[0, 4 * q:4 * q + 4, cols].bitcast(I32),
                                    in_=out_scales[32 * q:32 * q + 4, cols].bitcast(I32))

        make_identity(nc, ident32[:])
        make_identity(nc, ident16[:])
        nc.gpsimd.memset(ones16[:], 1.0)
        nc.vector.memset(bias_row[:], 0.0)
        nc.vector.memset(warm[:], 0.0)
        nc.scalar.activation(out=warm[:], in_=warm[:], func=ACT.Sigmoid)
        load_a(0, 0, 1)
        load_a(0, 1, 2)
        load_u(0, 0)
        load_a(0, 2, 3)
        load_a(0, 3, 4)
        load_w(0, 0)
        load_w(0, 1)
        load_u(0, 1)
        nc.sync.dma_start(out=bias_row[0:1, :], in_=bias.unsqueeze(0))
        load_x(0, 0, 2)
        load_w(1, 0)
        load_w(1, 1)
        load_u(0, 2)
        load_x(0, 2, 4)
        load_a(1, 0, 2)
        load_u(0, 3)
        load_w(2, 0)
        load_w(2, 1)
        load_a(1, 2, 4)
        load_u(1, 0)
        load_w(3, 0)
        load_w(3, 1)
        load_x(1, 0, 2)
        load_x(1, 2, 4)
        load_u(1, 1)

        turn("a", 0, 0, "turn0")
        turn("a", 0, 1, "h0")
        first_out("a", 0, False)
        u_interleave(0, 0, CH, True)
        first_out("a", 1, False)
        first_quant("a", 0)
        u_quant(0)
        first_quant("a", 1)
        turn("a", 0, 2, "h1")
        turn("a", 0, 3, "w1")
        stage1(0, 0)
        stage1(0, 1)
        w_to_psum(0)
        spread = bank("turn0", [P, F], BF16)
        for part in range(2):
            cols = slice(part * 512, (part + 1) * 512)
            nc.tensor.matmul(out=spread[:, cols], lhsT=ones16[:], rhs=bias_row[:, cols], start=True, stop=True)
        first_out("a", 2, False)
        first_out("a", 3, True)
        sigmoid(0, 0)
        sigmoid(0, 1)
        first_quant("a", 2)
        first_quant("a", 3)
        stage1(1, 0)
        stage1(1, 1)
        w_to_psum(1)
        u_interleave(1, 0, CH, True)
        gate_gpsimd(0)
        gate_vector(0)
        nc.vector.tensor_copy(out=bias_all[:], in_=spread[:])
        u_quant(1)
        step_quant(0, None)
        sigmoid(1, 0)
        sigmoid(1, 1)
        turn("x", 0, 0, "h0")
        turn("x", 0, 1, "h1")
        stage1(2, 0)
        stage1(2, 1)
        u_interleave(2, 0, CH, False)

        turns, outs = {}, {}
        for n in range(1, N):
            for i, kind in enumerate("aaaaxxxx"):
                leaves = STEPS_PER_SAMPLE * (n - 1) + 2 + i
                outs[leaves] = (kind, n, i % 4)
                turns.setdefault(leaves - i % RUN - T_LAST, []).append((kind, n, i % 4, "turn%d" % (i % RUN)))

        def live(s):
            return 0 <= s < STEPS

        for s in range(1, STEPS):
            if live(s + 1):
                w_to_psum(s + 1)
            if live(s - 3):
                stage2(s - 3)
            if s in outs and OUT_FIRST:
                turn_out(*outs[s], False, turned_region(s + 1))
            if live(s + 1):
                sigmoid(s + 1, 0)
                sigmoid(s + 1, 1)
            gate_gpsimd(s)
            if live(s - 4):
                add_bias(s - 4)
            gate_vector(s)
            for j in {1: (0, 1), 2: (2,), 3: (3,)}.get(s, ()):
                first_out("x", j, True)
            if not T_LAST:
                for args in turns.get(s, []):
                    turn(*args)
            if live(s + 2):
                stage1(s + 2, 0)
                stage1(s + 2, 1)
            if s == 1:
                turn("x", 0, 2, "h0")
                turn("x", 0, 3, "h1")
            if s % 2 == 0 and live(s + 4):
                split = U_VECTOR if s in outs and s > 3 else 0
                if split > 0:
                    u_interleave(s // 2 + 2, 0, split, True)
                if split < CH:
                    u_interleave(s // 2 + 2, split, CH, False)
            if s % 2 == 1 and live(s - 7):
                y_interleave((s - 7) // 2, 0, CH, False)
            if s in outs and not OUT_FIRST:
                turn_out(*outs[s], False, turned_region(s + 1))
            if T_LAST:
                for args in turns.get(s, []):
                    turn(*args)
            if s % 2 == 1 and live(s + 3):
                u_quant(s // 2 + 2)
            if s % 2 == 0 and live(s - 8):
                y_quant((s - 8) // 2, 0, CH)
            if s in (1, 2, 3):
                first_quant("x", (0, 2, 3)[s - 1])
            step_quant(s, outs.get(s - 1))
            if s == 1:
                first_quant("x", 1)
            if live(s - 4):
                leaky(s - 4, 0, CH)

            if s % 2 == 1 and live(s - 5):
                store_y((s - 5) // 2, 0, PACK)
            if s % 4 == 2 and live(s - 10):
                store_words((s - 10) // 2 * CH, (s - 6) // 2 * CH)

            ahead, phase = s // STEPS_PER_SAMPLE + 2, s % STEPS_PER_SAMPLE
            if ahead < N and phase == 5:
                load_a(ahead, 0, 2)
                load_a(ahead, 2, 4)
            if ahead < N and phase == 7:
                load_u(ahead, 0)
                load_u(ahead, 1)
            if 2 <= ahead - 1 < N and phase == 2:
                load_x(ahead - 1, 0, PACK)

        e, k, half = STEPS, STEPS // 2, CH // 2
        store_scales(0, k - 4, [nc.sync] * 4)
        stage2(e - 3)
        y_interleave(k - 3, 0, CH, False)
        add_bias(e - 4)
        stage2(e - 2)
        y_quant(k - 4, 0, CH)
        add_bias(e - 3)
        stage2(e - 1)
        leaky(e - 4, 0, CH)
        leaky(e - 3, 0, CH)
        store_y(k - 2, 0, PACK)
        y_interleave(k - 2, 0, CH, False)
        add_bias(e - 2)
        add_bias(e - 1)
        leaky(e - 2, 0, CH)
        store_y(k - 1, 0, 2)
        leaky(e - 1, 0, half)
        y_interleave(k - 1, 0, half, False)
        y_quant(k - 3, 0, CH)
        store_words((k - 4) * CH, (k - 2) * CH)
        leaky(e - 1, half, CH)
        store_y(k - 1, 2, PACK)
        y_quant(k - 2, 0, CH)
        y_interleave(k - 1, half, CH, True)
        y_quant(k - 1, 0, half)
        y_quant(k - 1, half, CH)
        store_words((k - 2) * CH, k * CH)
        store_scales(k - 4, k, [nc.scalar, nc.sync, nc.scalar, nc.sync])
